import numpy as np, ml_dtypes
CORES = [2,6,10,14,18,22,26,30]
N = 8
BF = ml_dtypes.bfloat16
def gentries(a):
    return np.ascontiguousarray(a.reshape(8, 16, -1).transpose(0, 2, 1)).reshape(8, -1)
def gtable(e):
    e = np.asarray(e); return np.ascontiguousarray(e.reshape(8, -1, 16).transpose(0, 2, 1)).reshape(128, -1).astype(np.int32)
def f(rng, *shape):
    return (rng.standard_normal(shape, dtype=np.float32) * np.exp2(rng.integers(-2, 3, shape[:-1] + (1,)))).astype(BF)
def wide(rng, *shape):
    v = f(rng, *shape).astype(np.float32); k = shape[:-2] + (1, shape[-1])
    return (v * np.exp2(rng.integers(-6, 7, k)) * (rng.random(k) > 0.0625)).astype(BF)
P, E, M, G = 2048, 4096, 512, 128
Z = P + (N - 1) * G
DX, DY = (-1, 0, 1, -1, 1, -1, 0, 1), (-1, -1, -1, 0, 0, 1, 1, 1)
FAR = [[(d, s) for d in range(8) for s in range(4) if max(abs(2 * DX[d] + s % 2 - c % 2), abs(2 * DY[d] + s // 2 - c // 2)) > 1] for c in range(4)]
def kids(rng):
    return rng.permuted(np.tile(np.minimum(np.arange(4 * P), E), (N, 8, 1)), axis=2).reshape(N, 8, 4, P)
def nears(rng, own, ghost):
    u = rng.random((N, 8, 8, M))
    return np.where(u < own, rng.integers(0, P, u.shape), np.where(u < own + ghost, rng.integers(P, Z, u.shape), Z))
def gives(rng):
    return rng.integers(0, P, (N, 8, N - 1, G))
def pack(rng, ki, ne, gi):
    return {"ex": f(rng, N, 128, E), "kid": ki.reshape(N, 8, 4 * P).astype(np.int32), "near": np.stack([gtable(a.reshape(8, 8 * M)) for a in ne]),
            "give": np.stack([gtable(a.reshape(8, (N - 1) * G)) for a in gi]), "tr": f(rng, N, 128, 108)}
def setup_inputs(rng):
    return pack(rng, kids(rng), nears(rng, 0.5, 0.42), gives(rng))
def setup_inputs_ghosts(rng):
    ne = nears(rng, 0.0, 2.0); q = rng.integers(0, N); ne[q] = P + G * rng.integers(0, N - 1) + rng.integers(0, G, (8, 8, M))
    for b in range(N - 1):
        ne[:, :, b, 0] = P + G * b; ne[:, :, b, M - 1] = P + G * b + G - 1
    return pack(rng, kids(rng), ne, gives(rng))
def setup_inputs_empty(rng):
    ne = nears(rng, 0.15, 0.15); ne[:, :, :, ::4] = Z; ne[:, rng.choice(np.array([0, 3, 4, 6, 7]))] = Z
    ki = kids(rng); ki[:, :, :, rng.random(P) < 0.5] = E; b = rng.integers(0, P)
    ki[:, :, :, b] = rng.integers(0, E, (N, 8, 4)); ne[:, 1:3, 0, 1] = b
    ne[:, 5, 7, 2] = b
    return pack(rng, ki, ne, gives(rng))
def setup_inputs_ends(rng):
    ne = rng.choice(np.array([0, P - 1, P, P + G - 1, Z - G, Z - 1, Z]), (N, 8, 8, M)); ki = kids(rng)
    for p in (0, P - 1): ki[:, :, :, p] = rng.permuted(np.tile(np.array([0, E - 1, E, E - 1]), (N, 8, 1)), axis=2)
    return pack(rng, ki, ne, rng.choice(np.array([0, P - 1]), (N, 8, N - 1, G)))
def setup_inputs_alike(rng):
    ne = np.tile(rng.integers(0, Z, (N, 8, 8, 1)), (1, 1, 1, M)); gi = np.tile(rng.integers(0, P, (N, 8, N - 1, 1)), (1, 1, 1, G))
    return pack(rng, rng.integers(0, E, (N, 8, 4, P)), ne, gi)
def setup_inputs_spread(rng):
    d = setup_inputs(rng); d["ex"] = wide(rng, N, 128, E); return d
def check_inputs(d):
    bad = []
    for a, top in (("kid", E), ("near", Z), ("give", P - 1)):
        if d[a].min() < 0 or d[a].max() > top: bad.append(a)
    for a in ("ex", "tr"):
        if not np.isfinite(d[a].astype(np.float32)).all(): bad.append(a)
    return bad
def reference(ex, kid, near, give, tr):
    x = np.concatenate([ex.astype(np.float64).reshape(N, 8, 16, E), np.zeros((N, 8, 16, 1))], 3)
    ch = kid.reshape(N, 8, 4, P); t = tr.astype(np.float64).reshape(N, 8, 16, 4, 27)
    gi = [gentries(a).reshape(8, N - 1, G) for a in give]; ne = [gentries(a).reshape(8, 8, M) for a in near]
    y = np.zeros((N, 8, 16, 4, M), np.float64)
    for r in range(N):
        for g in range(8):
            w = [x[r, g][:, ch[r, g]]]
            for d in range(1, N):
                q = (r - d) % N
                w.append(x[q, g][:, ch[q, g][:, gi[q][g, d - 1]]])
            w = np.concatenate(w + [np.zeros((16, 4, 1))], 2)
            v = w[:, :, ne[r][g]]
            for c in range(4):
                for i, (d, s) in enumerate(FAR[c]):
                    y[r, g, :, c] += t[r, g, :, c, i, None] * v[:, s, d]
    return {"y": y.reshape(N, 128, 4 * M).astype(np.float32)}

import numpy as np
from concourse.bass import DstId, RemoteDMATransfer
from concourse.mybir import dt, AluOpType, AxisListType, ActivationFunctionType

OP = AluOpType
COPY = ActivationFunctionType.Copy
N, P, E, M, G = 8, 2048, 4096, 512, 128
DX, DY = (-1, 0, 1, -1, 1, -1, 0, 1), (-1, -1, -1, 0, 0, 1, 1, 1)
FAR = [[(d, s) for d in range(8) for s in range(4)
        if max(abs(2 * DX[d] + s % 2 - c % 2), abs(2 * DY[d] + s // 2 - c // 2)) > 1] for c in range(4)]
XW = E + 16
GW = 2 * (N - 1) * G
TW = 2 * P + GW + 16

SCRATCH = {
    "kl": ("sbuf", [128, 512], "int32"), "ku": ("sbuf", [128, 512], "uint16"),
    "ni": ("sbuf", [128, 256], "int32"), "gi": ("sbuf", [128, 56], "int32"),
    "nf": ("sbuf", [128, 256], "float32"), "gf": ("sbuf", [128, 56], "float32"),
    "nu": ("sbuf", [128, 1024], "uint16"), "gu": ("sbuf", [128, 224], "uint16"),
    "im": ("sbuf", [128, 128], "int32"), "im2": ("sbuf", [128, 128], "int32"),
    "ip": ("sbuf", [128, 8], "int32"), "ip2": ("sbuf", [128, 8], "int32"), "cc": ("sbuf", [128, 8], "float32"),
    "rm": ("sbuf", [128, 128], "float32"), "em": ("sbuf", [128, 224], "bfloat16"),
    "tri": ("sbuf", [128, 108], "bfloat16"), "trf": ("sbuf", [128, 128], "bfloat16"),
    "trr": ("sbuf", [128, 128], "bfloat16"), "lt": ("sbuf", [128, 4096], "bfloat16"),
    "o": ("sbuf", [128, 2048], "float32"),
    "psy": ("psum", [128, 2048], "float32"), "psa": ("psum", [128, 2048], "float32"),
}
for _k in range(4):
    SCRATCH["xr%d" % _k] = ("sbuf", [128, XW], "bfloat16")
    SCRATCH["v%d" % _k] = ("sbuf", [128, 8 * M], "bfloat16")
for _h in range(2):
    SCRATCH["tab%d" % _h] = ("sbuf", [128, TW], "bfloat16")
    SCRATCH["gb%d" % _h] = ("sbuf", [128, GW], "bfloat16")
for _n in range(6):
    SCRATCH["na%d" % _n] = ("sbuf", [128, 256], "int32")
for _n in range(3):
    SCRATCH["ga%d" % _n] = ("sbuf", [128, 56], "int32")
SEMAPHORES = (["sv", "ss", "sp", "sg", "sent", "arr0", "arr1", "dg", "dn", "dt", "dy"]
              + ["dk%d" % k for k in range(4)] + ["dx%d" % k for k in range(4)])


def sends(q, cores, topo):
    me = cores[q]
    kinds = {"chip": [], "mate": [], "plane": [], "far": []}
    for d in range(1, N):
        c = cores[(q + d) % N]
        a, b = topo.chip(me), topo.chip(c)
        kinds["chip" if a == b else "mate" if topo.mates(a, b) else "plane" if topo.same_plane(a, b) else "far"].append((d, c))
    first = kinds["far"] + kinds["mate"][:1] + kinds["plane"][:1]
    second = kinds["mate"][1:] + kinds["plane"][1:]
    calls = []
    for group in (first, second):
        call = []
        for j, (d, c) in enumerate(group):
            eng = topo.engines(me, c)
            n = len(eng) // len(group)
            call.append((d, c, eng[n * j:n * j + n]))
        calls.append(call)
    used = set(topo.engines(me, first[0][1]))
    for d, c in kinds["chip"]:
        calls[1].append((d, c, [e for e in topo.engines(me, c) if e not in used]))
    return calls


def rank_program(g, core, T, topo):
    rank = T.rank_of(core)
    if rank is None:
        return
    cores = list(T.cores)
    V, S, PE, SY = g.vector, g.scalar, g.tensor, g.sync
    cnt = {"sv": 0, "ss": 0, "sp": 0, "sg": 0}
    seen = {}

    def inc(name, op):
        op.then_inc(T.sem[name], 1)
        cnt[name] += 1
        return cnt[name]

    def wait(qn, q, name, n):
        if seen.get((qn, name), 0) < n:
            q.wait_ge(T.sem[name], n)
            seen[(qn, name)] = n

    def vw(name, n):
        wait("V", V, name, n)

    def sw(name, n):
        wait("S", S, name, n)

    def pw(name, n):
        wait("P", PE, name, n)

    def load_k(q, k):
        for s in range(4):
            q.dma_start(T.kl[32 * s:32 * s + 32, 128 * k:128 * k + 128],
                        T.kid[2 * k:2 * k + 2, P * s:P * s + P]).then_inc(T.sem["dk%d" % k], 16)

    def load_x(q, k, ss):
        for s in ss:
            q.dma_start(T["xr%d" % k][32 * s:32 * s + 32, 0:E], T.ex[32 * k:32 * k + 32, :]).then_inc(T.sem["dx%d" % k], 16)

    S.dma_start(T.gi[:], T.give[:]).then_inc(T.sem.dg, 16)
    S.dma_start(T.ni[:], T.near[:]).then_inc(T.sem.dn, 16)
    load_k(SY, 0)
    load_x(SY, 0, (0, 1))
    load_x(S, 0, (2, 3))
    S.dma_start(T.tri[:], T.tr[:]).then_inc(T.sem.dt, 16)
    load_k(SY, 1)
    load_x(SY, 1, (0, 1))
    load_x(S, 1, (2, 3))
    for k in (2, 3):
        load_k(SY, k)
        load_x(SY, k, (0, 1, 2, 3))

    i1 = inc("sg", g.iota(T.im[:], [[-1, 128]], 128, 1))
    i2 = inc("sg", g.iota(T.ip[:], [[0, 8]], 0, 1))
    m_trf = inc("sv", V.memset(T.trf[:], 0.0))
    for k in range(4):
        m_x = inc("sv", V.memset(T["xr%d" % k][:, E:XW], 0.0))
    for h in range(2):
        m_t = inc("sv", V.memset(T["tab%d" % h][:, 2 * P + GW:TW], 0.0))
    m_em = inc("sv", V.memset(T.em[:], 0.0))
    vw("sg", i2)
    a = inc("sv", V.tensor_scalar(T.im2[:], T.im[:], 31, None, OP.bitwise_and))
    b = inc("sv", V.tensor_scalar(T.ip2[:], T.ip[:], 5, 1, OP.arith_shift_right, OP.bitwise_and))
    vw("sv", a)
    v_rm = inc("sv", V.tensor_scalar(T.rm[:], T.im2[:], 0, None, OP.is_equal))
    vw("sv", b)
    v_cc = inc("sv", V.tensor_scalar(T.cc[:], T.ip2[:], -2047, 2047, OP.mult, OP.add))
    vw("sv", v_rm)
    v_em = inc("sv", V.tensor_copy(T.em[:, 96:128], T.rm[:, 0:32]))

    sw("dt", 16)
    sw("sv", m_trf)
    for c in range(4):
        pos = [4 * d + s for d, s in FAR[c]]
        i = 0
        while i < 27:
            j = i
            while j + 1 < 27 and pos[j + 1] == pos[j] + 1:
                j += 1
            s_trf = inc("ss", S.activation(T.trf[:, 32 * c + pos[i]:32 * c + pos[j] + 1],
                                           T.tri[:, 27 * c + i:27 * c + j + 1], COPY))
            i = j + 1

    vw("dg", 16)
    g1 = inc("sv", V.tensor_scalar(T.ga0[:], T.gi[:], 16, None, OP.mult))
    g2 = inc("sv", V.tensor_scalar(T.ga1[:], T.gi[:], 7, None, OP.arith_shift_right))
    vw("dn", 16)
    n1 = inc("sv", V.tensor_scalar(T.na0[:], T.ni[:], P - 1, 16, OP.min, OP.mult))
    vw("sv", g2)
    g3 = inc("sv", V.tensor_scalar(T.ga2[:], T.ga1[:], -2047, None, OP.mult))
    n3 = inc("sv", V.tensor_scalar(T.na2[:], T.ni[:], P - 1, 2, OP.max, OP.mult))
    vw("sv", g3)
    g4 = inc("sv", V.tensor_tensor(T.gf[:], T.ga0[:], T.ga2[:], OP.add))
    n2 = inc("sv", V.tensor_scalar(T.na1[:], T.na0[:], 11, None, OP.arith_shift_right))
    n4 = inc("sv", V.tensor_scalar(T.na3[:], T.ni[:], P, T.cc[:, 0:1], OP.is_ge, OP.mult))
    vw("sv", n2)
    n5 = inc("sv", V.tensor_scalar(T.na4[:], T.na1[:], -2047, -4094, OP.mult, OP.add))
    vw("dk0", 64)
    v_ku = [inc("sv", V.tensor_copy(T.ku[:, 0:128], T.kl[:, 0:128]))]
    pw("sv", g4)
    for k in range(4):
        p_g = inc("sp", PE.matmul(T.psy[:, 512 * k:512 * k + 56], T.rm[32 * k:32 * k + 32, :], T.gf[32 * k:32 * k + 32, :], True, True))
    vw("sp", p_g)
    for k in range(4):
        v_gu = inc("sv", V.tensor_copy(T.gu[:, 56 * k:56 * k + 56], T.psy[:, 512 * k:512 * k + 56]))
    vw("sv", n4)
    n6 = inc("sv", V.tensor_tensor(T.na5[:], T.na0[:], T.na2[:], OP.add))
    vw("sv", n5)
    n7 = inc("sv", V.tensor_tensor(T.na1[:], T.na3[:], T.na4[:], OP.add))
    vw("sv", n7)
    n8 = inc("sv", V.tensor_tensor(T.nf[:], T.na5[:], T.na1[:], OP.add))
    pw("ss", s_trf)
    pw("sv", max(v_em, v_gu))
    for k in range(4):
        for s in range(4):
            op = PE.matmul(T.psy[:, 512 * k:512 * k + 32], T.em[32 * k:32 * k + 32, 96 - 32 * s:224 - 32 * s],
                           T.trf[32 * k:32 * k + 32, s::4], s == 0, s == 3)
            p_t = inc("sp", op)
    pw("sv", n8)
    for k in range(4):
        p_n = inc("sp", PE.matmul(T.psa[:, 512 * k:512 * k + 256], T.rm[32 * k:32 * k + 32, :], T.nf[32 * k:32 * k + 32, :], True, True))

    VC, GC = 64, 28
    done = {}

    def level1(k):
        h, j = k // 2, k % 2
        x, t = T["xr%d" % k], T["tab%d" % h]
        vw("dx%d" % k, 64)
        vw("sv", max(v_ku[k], m_x))
        lv = inc("sv", V.tensor_copy(t[:, P * j:P * j + 16 * VC], x[:, 0:XW].indirect(T.ku[:, 128 * k:128 * k + VC])))
        sw("dx%d" % k, 64)
        sw("sv", max(v_ku[k], m_x))
        ls = inc("ss", S.activation(t[:, P * j + 16 * VC:P * j + P], x[:, 0:XW].indirect(T.ku[:, 128 * k + VC:128 * k + 128]), COPY))
        done[k] = (lv, ls)

    def conv(k):
        vw("dk%d" % k, 64)
        v_ku.append(inc("sv", V.tensor_copy(T.ku[:, 128 * k:128 * k + 128], T.kl[:, 128 * k:128 * k + 128])))

    def ghosts(k):
        h, j = k // 2, k % 2
        t, b = T["tab%d" % h], T["gb%d" % h]
        lv, ls = done[k]
        w = t[:, P * j:P * j + P]
        vw("sv", max(lv, v_gu))
        vw("ss", ls)
        gv = inc("sv", V.tensor_copy(b[:, j:32 * GC:2], w.indirect(T.gu[:, 56 * k:56 * k + GC])))
        sw("ss", ls)
        sw("sv", max(lv, v_gu))
        gs = inc("ss", S.activation(b[:, 32 * GC + j:GW:2], w.indirect(T.gu[:, 56 * k + GC:56 * k + 56]), COPY))
        return gv, gs

    plan = sends(rank, cores, topo)
    sent = 0
    for h in range(2):
        for k in (2 * h, 2 * h + 1):
            if k:
                conv(k)
            level1(k)
            gv, gs = ghosts(k)
        g.wait_ge(T.sem.sv, gv)
        g.wait_ge(T.sem.ss, gs)
        b, t = T["gb%d" % h], T["tab%d" % h]
        for call in plan:
            tr = []
            for d, c, eng in call:
                ad = topo.addr(c)
                lo = 2 * G * (d - 1)
                tr.append(RemoteDMATransfer(dst_ids=[DstId(rid=ad[0], pnc=ad[1])], dma_engine_mask=sum(1 << e for e in eng),
                                            remote_sem=T.sem["arr%d" % h], src=b[:, lo:lo + 2 * G],
                                            dst=t[:, 2 * P + lo:2 * P + lo + 2 * G]))
                sent += len(eng)
            g.remote_dma_fused(tr, local_sem=T.sem.sent)

    vw("sp", p_t)
    for k in range(4):
        v_trr = inc("sv", V.tensor_copy(T.trr[:, k::4], T.psy[:, 512 * k:512 * k + 32]))
    vw("sp", p_n)
    v_nu = []
    for k in range(4):
        v_nu.append(inc("sv", V.tensor_copy(T.nu[:, 256 * k:256 * k + 256], T.psa[:, 512 * k:512 * k + 256])))
    vw("sv", v_trr)
    sw("sv", v_trr)
    for r in range(32):
        dst = T.lt[:, 128 * r:128 * r + 128]
        if r < 18:
            v_lt = inc("sv", V.tensor_scalar(dst, T.trr[:], T.rm[:, r:r + 1], None, OP.mult))
        else:
            s_lt = inc("ss", S.activation(dst, T.trr[:], COPY, scale=T.rm[:, r:r + 1]))

    arrive = 0
    for q in range(N):
        if q != rank:
            arrive += sum(len(e) for call in sends(q, cores, topo) for d, c, e in call if c == core)
    pw("sv", v_lt)
    pw("ss", s_lt)

    def evac(k, p):
        sw("sp", p)
        s = inc("ss", S.activation(T.o[:, 512 * k:512 * k + 512], T.psy[:, 512 * k:512 * k + 512], COPY))
        SY.wait_ge(T.sem.ss, s)
        SY.dma_start(T.y[32 * k:32 * k + 32, :], T.o[:, 512 * k:512 * k + 512]).then_inc(T.sem.dy, 16)

    pend = []
    for k in range(4):
        h, j = k // 2, k % 2
        win = T["tab%d" % h][:, P * j:TW]
        v = T["v%d" % k]
        vw("arr%d" % h, arrive)
        sw("arr%d" % h, arrive)
        vw("sv", v_nu[k])
        vw("ss", done[2 * h + 1][1])
        sw("sv", v_nu[k])
        w = 2 if k < 3 else 1
        for i, d in enumerate(range(0, 8, w)):
            src = win.indirect(T.nu[:, 256 * k + 32 * d:256 * k + 32 * (d + w)])
            dst = v[:, M * d:M * (d + w)]
            if i % 2 == 0:
                pw("sv", inc("sv", V.tensor_copy(dst, src)))
            else:
                pw("ss", inc("ss", S.activation(dst, src, COPY)))
            for e in range(d, d + w):
                lhs = T.lt[:, 4 * e + k::32]
                if k < 3:
                    p_y = inc("sp", PE.matmul(T.psy[:, 512 * k:512 * k + 512], lhs, v[:, M * e:M * e + M], e == 0, e == 7))
                else:
                    p_y = inc("sp", PE.matmul(T.psy[:, 1536:1792], lhs, v[:, M * e:M * e + 256], e == 0, e == 7))
                    p_y = inc("sp", PE.matmul(T.psa[:, 0:256], lhs, v[:, M * e + 256:M * e + M], e == 0, e == 7))
            if i == 1 and pend:
                evac(*pend.pop())
        pend.append((k, p_y))
    vw("sp", p_y - 1)
    ev = inc("sv", V.tensor_copy(T.o[:, 1536:1792], T.psy[:, 1536:1792]))
    sw("sp", p_y)
    es = inc("ss", S.activation(T.o[:, 1792:2048], T.psa[:, 0:256], COPY))
    SY.wait_ge(T.sem.sv, ev)
    SY.wait_ge(T.sem.ss, es)
    SY.dma_start(T.y[96:128, :], T.o[:, 1536:2048]).then_inc(T.sem.dy, 16)
    SY.wait_ge(T.sem.dy, 64)
    g.wait_ge(T.sem.sent, sent)
